import numpy as np, ml_dtypes
CORES = [125,127,253,255,381,383,509,511]
N = 8
import mx_ref
NC, G = 256, 2
C = np.float32(0.043)
CNT = [[24,64,32,80,0,24,16,16],[32,32,16,24,0,16,112,24],[0,16,88,16,120,0,0,16],[0,24,32,16,16,104,0,64],[48,24,0,16,64,16,56,32],[80,48,24,0,32,48,24,0],[72,32,48,64,24,0,0,16],[0,16,16,40,0,48,48,88]]
OFF = [[sum(c[:e]) for e in range(N + 1)] for c in CNT]
BF = ml_dtypes.bfloat16
def cut(t, i, w=512):
    return t[:, w * i:w * i + w]
def tile(rs):
    return np.stack(rs, axis=2).reshape(128, -1).astype(BF)
def layer(w, X):
    out = []
    for i in range(G):
        for t in range(len(X)):
            p = mx_ref.matmul(mx_ref.quantize(cut(w, len(X) * i + t)), X[t])
            z = p if t == 0 else z + p
        out.append(z)
    return out
def act(Z):
    return [np.maximum(s * z, 0) * C for z in Z for s in (1, -1)]
def setup_inputs(rng):
    def f(*shape):
        return mx_ref.flush((rng.standard_normal(shape, dtype=np.float32) * np.exp2(rng.integers(-2, 3, shape[:-1] + (1,)))).astype(BF))
    return {"x": f(N, 128, 4 * NC), "w1": f(N, 128, G * 512), "w2": f(N, 128, 512)}
def setup_inputs_blocks(rng):
    d = setup_inputs(rng)
    for k in ("x", "w1", "w2"): d[k] = mx_ref.spread(d[k], rng, 4)
    return d
def setup_inputs_wide(rng):
    d = setup_inputs(rng)
    for k in ("x", "w1", "w2"): d[k] = mx_ref.flush((d[k].astype(np.float32) * np.exp2(rng.integers(-8, 9, (N, 1, 1))).astype(np.float32)).astype(BF))
    return d
def setup_inputs_zeros(rng):
    d = setup_inputs(rng); v = d["x"].reshape(N, 128, -1, 4).copy()
    v[np.broadcast_to((rng.random((N, 1, v.shape[2], 1)) < 0.33), v.shape)] = 0
    d["x"] = v.reshape(d["x"].shape)
    return d
def reference(x, w1, w2):
    y = np.zeros((N, 128, NC), np.float32)
    for e in range(N):
        t = np.concatenate([x[j][:, 4 * OFF[j][e]:4 * OFF[j][e + 1]] for j in range(N)], axis=1)
        p = mx_ref.matmul(mx_ref.quantize(w2[e]), mx_ref.quantize(tile(act(layer(w1[e], [mx_ref.quantize(t)])))))
        y[e] = p
    return {"y": y}

@@ -1,0 +1,173 @@
+import numpy
+from concourse.mybir import dt, AluOpType, ActivationFunctionType
+
+COLS = 256
+WIN = 128
+SCALE = float(numpy.float32(0.043))
+
+SCRATCH = {
+    "xb": ("sbuf", [128, 4 * COLS], "bfloat16"),
+    "w1b": ("sbuf", [128, 1024], "bfloat16"),
+    "w2b": ("sbuf", [128, 512], "bfloat16"),
+    "xq": ("sbuf", [128, COLS], "float8_e4m3fn_x4"), "xs": ("sbuf", [128, COLS], "uint8"),
+    "w1q": ("sbuf", [128, 256], "float8_e4m3fn_x4"), "w1s": ("sbuf", [128, 256], "uint8"),
+    "w2q": ("sbuf", [128, 128], "float8_e4m3fn_x4"), "w2s": ("sbuf", [128, 128], "uint8"),
+    "bq": ("sbuf", [128, COLS], "float8_e4m3fn_x4"), "bs": ("sbuf", [128, COLS], "uint8"),
+    "tq": ("sbuf", [128, COLS], "float8_e4m3fn_x4"), "ts": ("sbuf", [128, COLS], "uint8"),
+    "hb": ("sbuf", [128, 4 * COLS], "bfloat16"),
+    "hq": ("sbuf", [128, COLS], "float8_e4m3fn_x4"), "hs": ("sbuf", [128, COLS], "uint8"),
+    "ob": ("sbuf", [128, 4 * WIN], "bfloat16"),
+    "ocq": ("sbuf", [128, WIN], "float8_e4m3fn_x4"), "ocs": ("sbuf", [128, WIN], "uint8"),
+    "yb": ("sbuf", [128, COLS], "float32"),
+    "mz0": ("psum", [128, 512], "float32"), "mz1": ("psum", [128, 512], "float32"), "mp": ("psum", [128, 512], "float32"),
+    "oz0": ("psum", [128, 512], "float32"), "oz1": ("psum", [128, 512], "float32"), "op": ("psum", [128, 512], "float32"),
+}
+SEMAPHORES = ["lx", "lw1", "lw2", "qx", "qw1", "qw2", "sent", "arr", "run",
+              "m0", "m1", "mh", "mq", "mpp", "o0", "o1", "oh", "oq", "opp", "yc", "st"]
+
+_CACHE = {}
+
+
+def _engines(mask):
+    return sum((mask >> b) & 1 for b in range(mask.bit_length()))
+
+
+def _plan(T, topo):
+    if "p" in _CACHE:
+        return _CACHE["p"]
+    cores = list(T.cores)
+    n = len(cores)
+    cnt = T.tables["CNT"]
+    off = [[sum(r[:e]) for e in range(n + 1)] for r in cnt]
+    pos = [[sum(cnt[i][e] for i in range(j) if i != e) for j in range(n)] for e in range(n)]
+    sends, due, taken = {}, {}, {}
+    buf = {"c": ("xq", "tq", "bq"), "s": ("xs", "ts", "bs")}
+
+    def one_chip(a, b):
+        return topo.host(a) == topo.host(b) and topo.chip(a) == topo.chip(b)
+
+    def put(src, kind, sb, a, w, dst, db, da, sem, mask):
+        if w == 0:
+            return
+        sends.setdefault(src, []).append((kind, sb, a, w, dst, db, da, sem, mask))
+        d = due.setdefault(dst, {})
+        d[sem] = d.get(sem, 0) + _engines(mask)
+
+    def on_chip_mask(src, dst, away):
+        return topo.mask(src, dst) & ~topo.mask(src, away)
+
+    for j, c in enumerate(cores):
+        others = [e for e in range(n) if e != j]
+        chip = [e for e in others if one_chip(c, cores[e])]
+        plane = [e for e in others if topo.same_plane(c, cores[e])]
+        cable = [e for e in others if e not in chip and e not in plane and topo.may_write(c, cores[e])]
+        far = sorted(cable + [e for e in others if not topo.may_write(c, cores[e])])
+        a, b = off[j][far[0]], off[j][far[-1] + 1]
+        assert far == list(range(far[0], far[-1] + 1))
+        gate = cores[cable[0]]
+        pool = [w for w in range(max(cores) + 1) if one_chip(w, gate) and w not in cores and topo.may_write(c, w)
+                and all(topo.may_write(w, cores[e]) for e in far)]
+        for kind in ("c", "s"):
+            pick = sorted((w for w in pool if w not in taken), key=lambda w: (topo.die(w) != topo.die(c), w))
+            relay = pick[0] if kind == "c" else pick[-1]
+            taken[relay] = True
+            xb, tb, lb = buf[kind]
+            put(c, kind, xb, a, b - a, relay, tb, 0, "run", topo.mask(c, relay))
+            away = [e for e in far if not one_chip(relay, cores[e])]
+            for e in away:
+                put(relay, kind, tb, off[j][e] - a, cnt[j][e], cores[e], lb, pos[e][j], "arr", topo.mask(relay, cores[e]))
+            for e in far:
+                if e not in away:
+                    put(relay, kind, tb, off[j][e] - a, cnt[j][e], cores[e], lb, pos[e][j], "arr",
+                        on_chip_mask(relay, cores[e], cores[away[0]]))
+        for e in plane:
+            for kind in ("c", "s"):
+                put(c, kind, buf[kind][0], off[j][e], cnt[j][e], cores[e], buf[kind][2], pos[e][j], "arr", topo.mask(c, cores[e]))
+        for e in chip:
+            for kind in ("c", "s"):
+                put(c, kind, buf[kind][0], off[j][e], cnt[j][e], cores[e], buf[kind][2], pos[e][j], "arr",
+                    on_chip_mask(c, cores[e], gate))
+    _CACHE["p"] = (sends, due, off)
+    return _CACHE["p"]
+
+
+def _send_all(g, core, T, topo, todo):
+    left = 0
+    for kind, sb, a, w, dst, db, da, sem, mask in todo:
+        src, out = T[sb][:, a:a + w], T[db][:, da:da + w]
+        if kind == "c":
+            src, out = src.bitcast(dt.uint8), out.bitcast(dt.uint8)
+        rid, pid = topo.addr(dst, core)
+        g.remote_dma(out_ap=out, in_ap=src, remote_sem=T.sem[sem], local_sem=T.sem.sent, pid=pid, routing_id=rid,
+                     dma_engine_mask=mask)
+        left += _engines(mask)
+    g.wait_ge(T.sem.sent, left)
+
+
+def _expert(g, T, p, rhs, rhs_s, n, z0, z1, hb, hq, hs, out):
+    S, te, ve, se = T.sem, g.tensor, g.vector, g.scalar
+    te.wait_ge(S.qw1, 1)
+    te.matmul_mx(z0[:, 0:n], T.w1q[:, 0:128], T.w1s[:, 0:128], rhs, rhs_s, True, True).then_inc(S[p + "0"], 1)
+    te.matmul_mx(z1[:, 0:n], T.w1q[:, 128:256], T.w1s[:, 128:256], rhs, rhs_s, True, True).then_inc(S[p + "1"], 1)
+    ve.wait_ge(S[p + "0"], 1)
+    ve.tensor_scalar(hb[:, 0:4 * n:4], z0[:, 0:n], SCALE, 0.0, AluOpType.mult, AluOpType.max).then_inc(S[p + "h"], 1)
+    ve.tensor_scalar(hb[:, 1:4 * n:4], z0[:, 0:n], -SCALE, 0.0, AluOpType.mult, AluOpType.max).then_inc(S[p + "h"], 1)
+    se.wait_ge(S[p + "1"], 1)
+    se.activation(hb[:, 2:4 * n:4], z1[:, 0:n], ActivationFunctionType.Relu, scale=SCALE).then_inc(S[p + "h"], 1)
+    se.activation(hb[:, 3:4 * n:4], z1[:, 0:n], ActivationFunctionType.Relu, scale=-SCALE).then_inc(S[p + "h"], 1)
+    ve.wait_ge(S[p + "h"], 4)
+    ve.quantize_mx(hq[:, 0:n], hs[:, 0:n], hb[:, 0:4 * n]).then_inc(S[p + "q"], 1)
+    te.wait_ge(S.qw2, 1)
+    te.wait_ge(S[p + "q"], 1)
+    te.matmul_mx(out[:, 0:n], T.w2q[:, 0:128], T.w2s[:, 0:128], hq[:, 0:n], hs[:, 0:n], True, True).then_inc(S[p + "pp"], 1)
+    ve.wait_ge(S[p + "pp"], 1)
+
+
+def rank_program(g, core, T, topo):
+    sends, due, off = _plan(T, topo)
+    S = T.sem
+    rank = T.rank_of(core)
+    if rank is None:
+        if core in sends:
+            g.wait_ge(S.run, due[core]["run"])
+            _send_all(g, core, T, topo, sends[core])
+        return
+
+    cnt = T.tables["CNT"]
+    own = cnt[rank][rank]
+    before = sum(cnt[i][rank] for i in range(rank))
+    landed = COLS - own
+
+    g.sync.dma_start(T.xb[:], T.x[:]).then_inc(S.lx, 16)
+    g.sync.dma_start(T.w1b[:], T.w1[:]).then_inc(S.lw1, 16)
+    g.sync.dma_start(T.w2b[:], T.w2[:]).then_inc(S.lw2, 16)
+    g.vector.wait_ge(S.lx, 16)
+    g.vector.quantize_mx(T.xq[:], T.xs[:], T.xb[:]).then_inc(S.qx, 1)
+    g.vector.wait_ge(S.lw1, 16)
+    g.vector.quantize_mx(T.w1q[:], T.w1s[:], T.w1b[:]).then_inc(S.qw1, 1)
+    g.vector.wait_ge(S.lw2, 16)
+    g.vector.quantize_mx(T.w2q[:], T.w2s[:], T.w2b[:]).then_inc(S.qw2, 1)
+
+    g.wait_ge(S.qx, 1)
+    _send_all(g, core, T, topo, sends[core])
+
+    copies = 0
+    if own:
+        assert own <= WIN
+        first = min(off[rank][rank], COLS - WIN)
+        g.tensor.wait_ge(S.qx, 1)
+        _expert(g, T, "o", T.xq[:, first:first + WIN], T.xs[:, first:first + WIN], WIN, T.oz0, T.oz1, T.ob, T.ocq, T.ocs, T.op)
+        at = off[rank][rank] - first
+        g.vector.tensor_copy(T.yb[:, before:before + own], T.op[:, at:at + own]).then_inc(S.yc, 1)
+        copies += 1
+    g.tensor.wait_ge(S.arr, due[core]["arr"])
+    _expert(g, T, "m", T.bq[:, 0:landed], T.bs[:, 0:landed], landed, T.mz0, T.mz1, T.hb, T.hq, T.hs, T.mp)
+    if before:
+        g.vector.tensor_copy(T.yb[:, 0:before], T.mp[:, 0:before]).then_inc(S.yc, 1)
+        copies += 1
+    if landed > before:
+        g.vector.tensor_copy(T.yb[:, before + own:COLS], T.mp[:, before:landed]).then_inc(S.yc, 1)
+        copies += 1
+    g.sync.wait_ge(S.yc, copies)
+    g.sync.dma_start(T.y[:], T.yb[:]).then_inc(S.st, 16)
+    g.sync.wait_ge(S.st, 16)

@@ -40,58 +40,45 @@ def _plan(T, topo):
     cnt = T.tables["CNT"]
     off = [[sum(r[:e]) for e in range(n + 1)] for r in cnt]
     pos = [[sum(cnt[i][e] for i in range(j) if i != e) for j in range(n)] for e in range(n)]
-    sends, due, taken = {}, {}, {}
+    sends, due = {c: [[], [], []] for c in cores}, {}
     buf = {"c": ("xq", "tq", "bq"), "s": ("xs", "ts", "bs")}
 
     def one_chip(a, b):
         return topo.host(a) == topo.host(b) and topo.chip(a) == topo.chip(b)
 
-    def put(src, kind, sb, a, w, dst, db, da, sem, mask):
+    def put(stage, src, kind, sb, a, w, dst, db, da, sem, mask):
         if w == 0:
             return
-        sends.setdefault(src, []).append((kind, sb, a, w, dst, db, da, sem, mask))
+        sends[src][stage].append((kind, sb, a, w, dst, db, da, sem, mask))
         d = due.setdefault(dst, {})
         d[sem] = d.get(sem, 0) + _engines(mask)
-
-    def on_chip_mask(src, dst, away):
-        return topo.mask(src, dst) & ~topo.mask(src, away)
 
     for j, c in enumerate(cores):
         others = [e for e in range(n) if e != j]
         chip = [e for e in others if one_chip(c, cores[e])]
         plane = [e for e in others if topo.same_plane(c, cores[e])]
         cable = [e for e in others if e not in chip and e not in plane and topo.may_write(c, cores[e])]
-        far = sorted(cable + [e for e in others if not topo.may_write(c, cores[e])])
-        a, b = off[j][far[0]], off[j][far[-1] + 1]
-        assert far == list(range(far[0], far[-1] + 1))
-        gate = cores[cable[0]]
-        pool = [w for w in range(max(cores) + 1) if one_chip(w, gate) and w not in cores and topo.may_write(c, w)
-                and all(topo.may_write(w, cores[e]) for e in far)]
+        diag = [e for e in others if not topo.may_write(c, cores[e])]
+        assert diag == list(range(diag[0], diag[-1] + 1))
+        a, b = off[j][diag[0]], off[j][diag[-1] + 1]
+        relay = cores[cable[sorted(chip + [j]).index(j) % len(cable)]]
         for kind in ("c", "s"):
-            pick = sorted((w for w in pool if w not in taken), key=lambda w: (topo.die(w) != topo.die(c), w))
-            relay = pick[0] if kind == "c" else pick[-1]
-            taken[relay] = True
             xb, tb, lb = buf[kind]
-            put(c, kind, xb, a, b - a, relay, tb, 0, "run", topo.mask(c, relay))
-            away = [e for e in far if not one_chip(relay, cores[e])]
-            for e in away:
-                put(relay, kind, tb, off[j][e] - a, cnt[j][e], cores[e], lb, pos[e][j], "arr", topo.mask(relay, cores[e]))
-            for e in far:
-                if e not in away:
-                    put(relay, kind, tb, off[j][e] - a, cnt[j][e], cores[e], lb, pos[e][j], "arr",
-                        on_chip_mask(relay, cores[e], cores[away[0]]))
-        for e in plane:
+            put(0, c, kind, xb, a, b - a, relay, tb, 0, "run", topo.mask(c, relay))
+        for e in diag:
             for kind in ("c", "s"):
-                put(c, kind, buf[kind][0], off[j][e], cnt[j][e], cores[e], buf[kind][2], pos[e][j], "arr", topo.mask(c, cores[e]))
-        for e in chip:
-            for kind in ("c", "s"):
-                put(c, kind, buf[kind][0], off[j][e], cnt[j][e], cores[e], buf[kind][2], pos[e][j], "arr",
-                    on_chip_mask(c, cores[e], gate))
+                xb, tb, lb = buf[kind]
+                put(1, relay, kind, tb, off[j][e] - a, cnt[j][e], cores[e], lb, pos[e][j], "arr", topo.mask(relay, cores[e]))
+        for stage, group in ((0, cable), (0, plane), (2, chip)):
+            for e in group:
+                for kind in ("c", "s"):
+                    put(stage, c, kind, buf[kind][0], off[j][e], cnt[j][e], cores[e], buf[kind][2], pos[e][j], "arr",
+                        topo.mask(c, cores[e]) & topo.mask(c, relay))
     _CACHE["p"] = (sends, due, off)
     return _CACHE["p"]
 
 
-def _send_all(g, core, T, topo, todo):
+def _send(g, core, T, topo, todo):
     left = 0
     for kind, sb, a, w, dst, db, da, sem, mask in todo:
         src, out = T[sb][:, a:a + w], T[db][:, da:da + w]
@@ -101,7 +88,7 @@ def _send_all(g, core, T, topo, todo):
         g.remote_dma(out_ap=out, in_ap=src, remote_sem=T.sem[sem], local_sem=T.sem.sent, pid=pid, routing_id=rid,
                      dma_engine_mask=mask)
         left += _engines(mask)
-    g.wait_ge(T.sem.sent, left)
+    return left
 
 
 def _expert(g, T, p, rhs, rhs_s, n, z0, z1, hb, hq, hs, out):
@@ -124,15 +111,11 @@ def _expert(g, T, p, rhs, rhs_s, n, z0, z1, hb, hq, hs, out):
 
 
 def rank_program(g, core, T, topo):
-    sends, due, off = _plan(T, topo)
-    S = T.sem
     rank = T.rank_of(core)
     if rank is None:
-        if core in sends:
-            g.wait_ge(S.run, due[core]["run"])
-            _send_all(g, core, T, topo, sends[core])
         return
-
+    sends, due, off = _plan(T, topo)
+    S = T.sem
     cnt = T.tables["CNT"]
     own = cnt[rank][rank]
     before = sum(cnt[i][rank] for i in range(rank))
@@ -149,7 +132,12 @@ def rank_program(g, core, T, topo):
     g.vector.quantize_mx(T.w2q[:], T.w2s[:], T.w2b[:]).then_inc(S.qw2, 1)
 
     g.wait_ge(S.qx, 1)
-    _send_all(g, core, T, topo, sends[core])
+    left = _send(g, core, T, topo, sends[core][0])
+    if sends[core][1]:
+        g.wait_ge(S.run, due[core]["run"])
+        left += _send(g, core, T, topo, sends[core][1])
+    left += _send(g, core, T, topo, sends[core][2])
+    g.wait_ge(S.sent, left)
 
     copies = 0
     if own:

@@ -13,17 +13,20 @@ SCRATCH = {
     "w1q": ("sbuf", [128, 256], "float8_e4m3fn_x4"), "w1s": ("sbuf", [128, 256], "uint8"),
     "w2q": ("sbuf", [128, 128], "float8_e4m3fn_x4"), "w2s": ("sbuf", [128, 128], "uint8"),
     "bq": ("sbuf", [128, COLS], "float8_e4m3fn_x4"), "bs": ("sbuf", [128, COLS], "uint8"),
-    "tq": ("sbuf", [128, COLS], "float8_e4m3fn_x4"), "ts": ("sbuf", [128, COLS], "uint8"),
+    "tq": ("sbuf", [128, 4 * COLS], "float8_e4m3fn_x4"), "ts": ("sbuf", [128, 4 * COLS], "uint8"),
     "hb": ("sbuf", [128, 4 * COLS], "bfloat16"),
     "hq": ("sbuf", [128, COLS], "float8_e4m3fn_x4"), "hs": ("sbuf", [128, COLS], "uint8"),
+    "lb": ("sbuf", [128, 4 * COLS], "bfloat16"),
+    "lcq": ("sbuf", [128, COLS], "float8_e4m3fn_x4"), "lcs": ("sbuf", [128, COLS], "uint8"),
     "ob": ("sbuf", [128, 4 * WIN], "bfloat16"),
     "ocq": ("sbuf", [128, WIN], "float8_e4m3fn_x4"), "ocs": ("sbuf", [128, WIN], "uint8"),
     "yb": ("sbuf", [128, COLS], "float32"),
     "mz0": ("psum", [128, 512], "float32"), "mz1": ("psum", [128, 512], "float32"), "mp": ("psum", [128, 512], "float32"),
     "oz0": ("psum", [128, 512], "float32"), "oz1": ("psum", [128, 512], "float32"), "op": ("psum", [128, 512], "float32"),
+    "lp": ("psum", [128, 512], "float32"),
 }
-SEMAPHORES = ["lx", "lw1", "lw2", "qx", "qw1", "qw2", "sent", "arr", "run",
-              "m0", "m1", "mh", "mq", "mpp", "o0", "o1", "oh", "oq", "opp", "yc", "st"]
+SEMAPHORES = ["lx", "lw1", "lw2", "qx", "qw1", "qw2", "sent", "arr", "arl", "run",
+              "m0", "m1", "mh", "mq", "mpp", "o0", "o1", "oh", "oq", "opp", "v0", "v1", "vh", "vq", "vpp", "yc", "st"]
 
 _CACHE = {}
 
@@ -39,7 +42,15 @@ def _plan(T, topo):
     n = len(cores)
     cnt = T.tables["CNT"]
     off = [[sum(r[:e]) for e in range(n + 1)] for r in cnt]
-    pos = [[sum(cnt[i][e] for i in range(j) if i != e) for j in range(n)] for e in range(n)]
+    late = [[j for j in range(n) if j != e and cnt[j][e] and not topo.may_write(cores[j], cores[e])] for e in range(n)]
+    pos = []
+    for e in range(n):
+        order = [j for j in range(n) if j != e and j not in late[e]] + late[e]
+        at, row = 0, [0] * n
+        for j in order:
+            row[j] = at
+            at += cnt[j][e]
+        pos.append(row)
     sends, due = {c: [[], [], []] for c in cores}, {}
     buf = {"c": ("xq", "tq", "bq"), "s": ("xs", "ts", "bs")}
 
@@ -53,28 +64,56 @@ def _plan(T, topo):
         d = due.setdefault(dst, {})
         d[sem] = d.get(sem, 0) + _engines(mask)
 
+    groups = []
     for j, c in enumerate(cores):
         others = [e for e in range(n) if e != j]
         chip = [e for e in others if one_chip(c, cores[e])]
-        plane = [e for e in others if topo.same_plane(c, cores[e])]
-        cable = [e for e in others if e not in chip and e not in plane and topo.may_write(c, cores[e])]
         diag = [e for e in others if not topo.may_write(c, cores[e])]
+        straight = [e for e in others if e not in chip and e not in diag]
         assert diag == list(range(diag[0], diag[-1] + 1))
-        a, b = off[j][diag[0]], off[j][diag[-1] + 1]
-        relay = cores[cable[sorted(chip + [j]).index(j) % len(cable)]]
-        for kind in ("c", "s"):
-            xb, tb, lb = buf[kind]
-            put(0, c, kind, xb, a, b - a, relay, tb, 0, "run", topo.mask(c, relay))
-        for e in diag:
+        straight.sort(key=lambda e: (topo.same_plane(c, cores[e]), e))
+        groups.append((chip, diag, straight))
+    load = [2 * sum(1 for e in groups[j][2] if cnt[j][e]) + 2 * (1 if any(cnt[j][e] for e in groups[j][1]) else 0)
+            for j in range(n)]
+    relay_of, room = {}, [0] * n
+    todo = sorted(range(n), key=lambda j: (-sum(1 for e in groups[j][1] if cnt[j][e]), j))
+    for j in todo:
+        chip, diag, straight = groups[j]
+        pieces = 2 * sum(1 for e in diag if cnt[j][e])
+        if not pieces:
+            continue
+        can = [r for r in straight if all(topo.may_write(cores[r], cores[e]) for e in diag)]
+        r = min(can, key=lambda r: (load[r], topo.same_plane(cores[j], cores[r]), r))
+        relay_of[j] = r
+        load[r] += pieces
+
+    for j, c in enumerate(cores):
+        chip, diag, straight = groups[j]
+        far = topo.mask(c, cores[straight[0]])
+        if j in relay_of:
+            r = relay_of[j]
+            relay = cores[r]
+            live = [e for e in diag if cnt[j][e]]
+            a, b = off[j][live[0]], off[j][live[-1] + 1]
+            base = room[r]
+            room[r] += b - a
+            assert room[r] <= 4 * COLS
             for kind in ("c", "s"):
-                xb, tb, lb = buf[kind]
-                put(1, relay, kind, tb, off[j][e] - a, cnt[j][e], cores[e], lb, pos[e][j], "arr", topo.mask(relay, cores[e]))
-        for stage, group in ((0, cable), (0, plane), (2, chip)):
-            for e in group:
+                put(0, c, kind, buf[kind][0], a, b - a, relay, buf[kind][1], base, "run", topo.mask(c, relay))
+            for e in live:
                 for kind in ("c", "s"):
-                    put(stage, c, kind, buf[kind][0], off[j][e], cnt[j][e], cores[e], buf[kind][2], pos[e][j], "arr",
-                        topo.mask(c, cores[e]) & topo.mask(c, relay))
-    _CACHE["p"] = (sends, due, off)
+                    put(2, relay, kind, buf[kind][1], base + off[j][e] - a, cnt[j][e], cores[e], buf[kind][2], pos[e][j], "arl",
+                        topo.mask(relay, cores[e]))
+        for e in straight:
+            for kind in ("c", "s"):
+                put(0, c, kind, buf[kind][0], off[j][e], cnt[j][e], cores[e], buf[kind][2], pos[e][j], "arr",
+                    topo.mask(c, cores[e]))
+        for e in chip:
+            near = topo.mask(c, cores[e]) & ~far
+            for kind in ("c", "s"):
+                put(1, c, kind, buf[kind][0], off[j][e], cnt[j][e], cores[e], buf[kind][2], pos[e][j], "arr",
+                    near if near else topo.mask(c, cores[e]))
+    _CACHE["p"] = (sends, due, off, pos, late)
     return _CACHE["p"]
 
 
@@ -110,16 +149,34 @@ def _expert(g, T, p, rhs, rhs_s, n, z0, z1, hb, hq, hs, out):
     ve.wait_ge(S[p + "pp"], 1)
 
 
+def _pieces(ranks, cnt, e, pos, shift):
+    out = []
+    for j in ranks:
+        w = cnt[j][e]
+        if not w:
+            continue
+        ya, sa = sum(cnt[i][e] for i in range(j)), pos[e][j] - shift
+        if out and out[-1][0] + out[-1][2] == ya and out[-1][1] + out[-1][2] == sa:
+            out[-1] = (out[-1][0], out[-1][1], out[-1][2] + w)
+        else:
+            out.append((ya, sa, w))
+    return out
+
+
 def rank_program(g, core, T, topo):
     rank = T.rank_of(core)
     if rank is None:
         return
-    sends, due, off = _plan(T, topo)
+    sends, due, off, pos, late = _plan(T, topo)
     S = T.sem
     cnt = T.tables["CNT"]
+    n = len(cnt)
     own = cnt[rank][rank]
     before = sum(cnt[i][rank] for i in range(rank))
     landed = COLS - own
+    tail = sum(cnt[j][rank] for j in late[rank])
+    head = landed - tail
+    early = [j for j in range(n) if j != rank and j not in late[rank]]
 
     g.sync.dma_start(T.xb[:], T.x[:]).then_inc(S.lx, 16)
     g.sync.dma_start(T.w1b[:], T.w1[:]).then_inc(S.lw1, 16)
@@ -133,10 +190,10 @@ def rank_program(g, core, T, topo):
 
     g.wait_ge(S.qx, 1)
     left = _send(g, core, T, topo, sends[core][0])
-    if sends[core][1]:
+    left += _send(g, core, T, topo, sends[core][1])
+    if sends[core][2]:
         g.wait_ge(S.run, due[core]["run"])
-        left += _send(g, core, T, topo, sends[core][1])
-    left += _send(g, core, T, topo, sends[core][2])
+        left += _send(g, core, T, topo, sends[core][2])
     g.wait_ge(S.sent, left)
 
     copies = 0
@@ -149,13 +206,25 @@ def rank_program(g, core, T, topo):
         g.vector.tensor_copy(T.yb[:, before:before + own], T.op[:, at:at + own]).then_inc(S.yc, 1)
         copies += 1
     g.tensor.wait_ge(S.arr, due[core]["arr"])
-    _expert(g, T, "m", T.bq[:, 0:landed], T.bs[:, 0:landed], landed, T.mz0, T.mz1, T.hb, T.hq, T.hs, T.mp)
-    if before:
-        g.vector.tensor_copy(T.yb[:, 0:before], T.mp[:, 0:before]).then_inc(S.yc, 1)
-        copies += 1
-    if landed > before:
-        g.vector.tensor_copy(T.yb[:, before + own:COLS], T.mp[:, before:landed]).then_inc(S.yc, 1)
-        copies += 1
+    if tail and head >= WIN:
+        _expert(g, T, "m", T.bq[:, 0:head], T.bs[:, 0:head], head, T.mz0, T.mz1, T.hb, T.hq, T.hs, T.mp)
+        for ya, sa, w in _pieces(early, cnt, rank, pos, 0):
+            g.vector.tensor_copy(T.yb[:, ya:ya + w], T.mp[:, sa:sa + w]).then_inc(S.yc, 1)
+            copies += 1
+        wide = max(WIN, tail)
+        a = landed - wide
+        g.tensor.wait_ge(S.arl, due[core]["arl"])
+        _expert(g, T, "v", T.bq[:, a:landed], T.bs[:, a:landed], wide, T.oz0, T.oz1, T.lb, T.lcq, T.lcs, T.lp)
+        for ya, sa, w in _pieces(late[rank], cnt, rank, pos, a):
+            g.vector.tensor_copy(T.yb[:, ya:ya + w], T.lp[:, sa:sa + w]).then_inc(S.yc, 1)
+            copies += 1
+    else:
+        if tail:
+            g.tensor.wait_ge(S.arl, due[core]["arl"])
+        _expert(g, T, "m", T.bq[:, 0:landed], T.bs[:, 0:landed], landed, T.mz0, T.mz1, T.hb, T.hq, T.hs, T.mp)
+        for ya, sa, w in _pieces(early + late[rank], cnt, rank, pos, 0):
+            g.vector.tensor_copy(T.yb[:, ya:ya + w], T.mp[:, sa:sa + w]).then_inc(S.yc, 1)
+            copies += 1
     g.sync.wait_ge(S.yc, copies)
     g.sync.dma_start(T.y[:], T.yb[:]).then_inc(S.st, 16)
     g.sync.wait_ge(S.st, 16)

@@ -1,4 +1,5 @@
 import numpy
+from concourse.bass import DstId, RemoteDMATransfer
 from concourse.mybir import dt, AluOpType, ActivationFunctionType
 
 COLS = 256
@@ -6,6 +7,8 @@ WIN = 128
 SCALE = float(numpy.float32(0.043))
 
 SCRATCH = {
+    "ab": ("sbuf", [128, 4 * WIN], "bfloat16"),
+    "aq": ("sbuf", [128, WIN], "float8_e4m3fn_x4"), "asc": ("sbuf", [128, WIN], "uint8"),
     "xb": ("sbuf", [128, 4 * COLS], "bfloat16"),
     "w1b": ("sbuf", [128, 1024], "bfloat16"),
     "w2b": ("sbuf", [128, 512], "bfloat16"),
@@ -25,14 +28,47 @@ SCRATCH = {
     "oz0": ("psum", [128, 512], "float32"), "oz1": ("psum", [128, 512], "float32"), "op": ("psum", [128, 512], "float32"),
     "lp": ("psum", [128, 512], "float32"),
 }
-SEMAPHORES = ["lx", "lw1", "lw2", "qx", "qw1", "qw2", "sent", "arr", "arl", "run",
-              "m0", "m1", "mh", "mq", "mpp", "o0", "o1", "oh", "oq", "opp", "v0", "v1", "vh", "vq", "vpp", "yc", "st"]
+RUNS = 4
+SEMAPHORES = ["la", "lx", "lw1", "lw2", "qa", "qx", "qw1", "qw2", "sent", "arr", "arl", "zl"] + [
+              "r%s%d" % (t, k) for k in range(RUNS) for t in "cs"] + [
+              "m0", "m1", "mh", "mq", "mpp", "o0", "o1", "oh", "oq", "opp", "v0", "v1", "vh", "vq", "vpp", "ye", "yc", "se", "st"]
 
 _CACHE = {}
 
 
 def _engines(mask):
     return sum((mask >> b) & 1 for b in range(mask.bit_length()))
+
+
+def _halves(mask):
+    bits = [b for b in range(mask.bit_length()) if (mask >> b) & 1]
+    half = len(bits) // 2
+    return [sum(1 << b for b in bits[:half]), sum(1 << b for b in bits[half:])]
+
+
+def _width(t):
+    return t[3] * (4 if t[0] == "c" else 1)
+
+
+def _fuse(todo):
+    calls, used = [], set()
+    for i in range(len(todo) - 1, -1, -1):
+        if i in used:
+            continue
+        by = {}
+        for k in range(i, -1, -1):
+            m = todo[k][8]
+            if k in used or _width(todo[k]) != _width(todo[i]) or any(m != o and m & o for o in by):
+                continue
+            if len(by.setdefault(m, [])) < 2:
+                by[m].append(k)
+        call = []
+        for m, ks in by.items():
+            for k, part in zip(ks, _halves(m) if len(ks) == 2 else [m]):
+                call.append(todo[k][:8] + (part,))
+                used.add(k)
+        calls.append(call)
+    return calls[::-1]
 
 
 def _plan(T, topo):
@@ -42,27 +78,41 @@ def _plan(T, topo):
     n = len(cores)
     cnt = T.tables["CNT"]
     off = [[sum(r[:e]) for e in range(n + 1)] for r in cnt]
-    late = [[j for j in range(n) if j != e and cnt[j][e] and not topo.may_write(cores[j], cores[e])] for e in range(n)]
-    pos = []
-    for e in range(n):
-        order = [j for j in range(n) if j != e and j not in late[e]] + late[e]
-        at, row = 0, [0] * n
-        for j in order:
-            row[j] = at
-            at += cnt[j][e]
-        pos.append(row)
-    sends, due = {c: [[], [], []] for c in cores}, {}
-    buf = {"c": ("xq", "tq", "bq"), "s": ("xs", "ts", "bs")}
 
     def one_chip(a, b):
         return topo.host(a) == topo.host(b) and topo.chip(a) == topo.chip(b)
 
-    def put(stage, src, kind, sb, a, w, dst, db, da, sem, mask):
+    late = [[j for j in range(n) if j != e and cnt[j][e] and not topo.may_write(cores[j], cores[e])] for e in range(n)]
+    pos, pad, wide = [], [0] * n, {}
+    for e in range(n):
+        near = [j for j in range(n) if j != e and j not in late[e] and one_chip(cores[j], cores[e]) and cnt[j][e]]
+        first = [j for j in range(n) if j != e and j not in late[e] and j not in near]
+        head = sum(cnt[j][e] for j in first + near)
+        if late[e] and head < WIN and near:
+            pad[e] = WIN - head
+        at, row = 0, [0] * n
+        for j in first + near + late[e]:
+            row[j] = at
+            if pad[e] and j == near[-1]:
+                w = cnt[j][e] + pad[e]
+                if off[j][e] + w <= COLS:
+                    wide[(j, e)] = (off[j][e], w, at)
+                else:
+                    assert off[j][e + 1] - w >= 0
+                    wide[(j, e)] = (off[j][e + 1] - w, w, at)
+                    row[j] = at + pad[e]
+                at += w
+            else:
+                at += cnt[j][e]
+        assert at <= COLS
+        pos.append(row)
+    sends, relays, due = {c: [[], [], []] for c in cores}, {c: [] for c in cores}, {}
+    buf = {"c": ("xq", "tq", "bq", "aq"), "s": ("xs", "ts", "bs", "asc")}
+
+    def put(todo, kind, sb, a, w, dst, db, da, sem, mask):
         if w == 0:
             return
-        sends[src][stage].append((kind, sb, a, w, dst, db, da, sem, mask))
-        d = due.setdefault(dst, {})
-        d[sem] = d.get(sem, 0) + _engines(mask)
+        todo.append((kind, sb, a, w, dst, db, da, sem, mask))
 
     groups = []
     for j, c in enumerate(cores):
@@ -87,6 +137,7 @@ def _plan(T, topo):
         relay_of[j] = r
         load[r] += pieces
 
+    win = [None] * n
     for j, c in enumerate(cores):
         chip, diag, straight = groups[j]
         far = topo.mask(c, cores[straight[0]])
@@ -95,52 +146,76 @@ def _plan(T, topo):
             relay = cores[r]
             live = [e for e in diag if cnt[j][e]]
             a, b = off[j][live[0]], off[j][live[-1] + 1]
+            assert b - a <= WIN
+            win[j] = min(a, COLS - WIN)
             base = room[r]
             room[r] += b - a
-            assert room[r] <= 4 * COLS
+            assert room[r] <= 4 * COLS and len(relays[relay]) < RUNS
+            slot = len(relays[relay])
             for kind in ("c", "s"):
-                put(0, c, kind, buf[kind][0], a, b - a, relay, buf[kind][1], base, "run", topo.mask(c, relay))
-            for e in live:
+                put(sends[c][0], kind, buf[kind][3], a - win[j], b - a, relay, buf[kind][1], base, "r%s%d" % (kind, slot),
+                    topo.mask(c, relay))
+            on = []
+            for e in sorted(live, key=lambda e: (-sum(cnt[i][e] for i in late[e]), e)):
                 for kind in ("c", "s"):
-                    put(2, relay, kind, buf[kind][1], base + off[j][e] - a, cnt[j][e], cores[e], buf[kind][2], pos[e][j], "arl",
+                    put(on, kind, buf[kind][1], base + off[j][e] - a, cnt[j][e], cores[e], buf[kind][2], pos[e][j], "arl",
                         topo.mask(relay, cores[e]))
+            relays[relay].append((b - a, slot, [("rc%d" % slot, [[t] for t in on[:1]]), ("rs%d" % slot, [[t] for t in on[1:]])]))
         for e in straight:
             for kind in ("c", "s"):
-                put(0, c, kind, buf[kind][0], off[j][e], cnt[j][e], cores[e], buf[kind][2], pos[e][j], "arr",
+                put(sends[c][1], kind, buf[kind][0], off[j][e], cnt[j][e], cores[e], buf[kind][2], pos[e][j], "arr",
                     topo.mask(c, cores[e]))
         for e in chip:
             near = topo.mask(c, cores[e]) & ~far
+            a, w, da = wide.get((j, e), (off[j][e], cnt[j][e], pos[e][j]))
             for kind in ("c", "s"):
-                put(1, c, kind, buf[kind][0], off[j][e], cnt[j][e], cores[e], buf[kind][2], pos[e][j], "arr",
+                put(sends[c][2], kind, buf[kind][0], a, w, cores[e], buf[kind][2], da, "arr",
                     near if near else topo.mask(c, cores[e]))
-    _CACHE["p"] = (sends, due, off, pos, late)
+    for c in cores:
+        relays[c].sort(key=lambda t: (t[0], t[1]))
+        sends[c] = [[[t] for t in sends[c][0]], _fuse(sends[c][1] + sends[c][2])]
+        for calls in sends[c] + [s[1] for r in relays[c] for s in r[2]]:
+            for call in calls:
+                for t in call:
+                    d = due.setdefault(t[4], {})
+                    d[t[7]] = d.get(t[7], 0) + _engines(t[8])
+    _CACHE["p"] = (sends, relays, due, off, pos, late, pad, win)
     return _CACHE["p"]
 
 
-def _send(g, core, T, topo, todo):
+def _send(g, core, T, topo, calls):
     left = 0
-    for kind, sb, a, w, dst, db, da, sem, mask in todo:
-        src, out = T[sb][:, a:a + w], T[db][:, da:da + w]
-        if kind == "c":
-            src, out = src.bitcast(dt.uint8), out.bitcast(dt.uint8)
-        rid, pid = topo.addr(dst, core)
-        g.remote_dma(out_ap=out, in_ap=src, remote_sem=T.sem[sem], local_sem=T.sem.sent, pid=pid, routing_id=rid,
-                     dma_engine_mask=mask)
-        left += _engines(mask)
+    for call in calls:
+        parts = []
+        for kind, sb, a, w, dst, db, da, sem, mask in call:
+            src, out = T[sb][:, a:a + w], T[db][:, da:da + w]
+            if kind == "c":
+                src, out = src.bitcast(dt.uint8), out.bitcast(dt.uint8)
+            rid, pid = topo.addr(dst, core)
+            parts.append((src, out, rid, pid, T.sem[sem], mask))
+            left += _engines(mask)
+        if len(parts) == 1:
+            src, out, rid, pid, sem, mask = parts[0]
+            g.remote_dma(out_ap=out, in_ap=src, remote_sem=sem, local_sem=T.sem.sent, pid=pid, routing_id=rid,
+                         dma_engine_mask=mask)
+        else:
+            g.remote_dma_fused([RemoteDMATransfer(dst_ids=[DstId(rid=rid, pnc=pid)], dma_engine_mask=mask, remote_sem=sem,
+                                                  src=src, dst=out) for src, out, rid, pid, sem, mask in parts],
+                               local_sem=T.sem.sent)
     return left
 
 
-def _expert(g, T, p, rhs, rhs_s, n, z0, z1, hb, hq, hs, out):
+def _expert(g, T, p, rhs, rhs_s, n, z0, z1, hb, hq, hs, out, k=0):
     S, te, ve, se = T.sem, g.tensor, g.vector, g.scalar
     te.wait_ge(S.qw1, 1)
     te.matmul_mx(z0[:, 0:n], T.w1q[:, 0:128], T.w1s[:, 0:128], rhs, rhs_s, True, True).then_inc(S[p + "0"], 1)
     te.matmul_mx(z1[:, 0:n], T.w1q[:, 128:256], T.w1s[:, 128:256], rhs, rhs_s, True, True).then_inc(S[p + "1"], 1)
     ve.wait_ge(S[p + "0"], 1)
-    ve.tensor_scalar(hb[:, 0:4 * n:4], z0[:, 0:n], SCALE, 0.0, AluOpType.mult, AluOpType.max).then_inc(S[p + "h"], 1)
-    ve.tensor_scalar(hb[:, 1:4 * n:4], z0[:, 0:n], -SCALE, 0.0, AluOpType.mult, AluOpType.max).then_inc(S[p + "h"], 1)
+    ve.tensor_scalar(hb[:, 4 * k:4 * n:4], z0[:, k:n], SCALE, 0.0, AluOpType.mult, AluOpType.max).then_inc(S[p + "h"], 1)
+    ve.tensor_scalar(hb[:, 4 * k + 1:4 * n:4], z0[:, k:n], -SCALE, 0.0, AluOpType.mult, AluOpType.max).then_inc(S[p + "h"], 1)
     se.wait_ge(S[p + "1"], 1)
-    se.activation(hb[:, 2:4 * n:4], z1[:, 0:n], ActivationFunctionType.Relu, scale=SCALE).then_inc(S[p + "h"], 1)
-    se.activation(hb[:, 3:4 * n:4], z1[:, 0:n], ActivationFunctionType.Relu, scale=-SCALE).then_inc(S[p + "h"], 1)
+    se.activation(hb[:, 4 * k + 2:4 * n:4], z1[:, k:n], ActivationFunctionType.Relu, scale=SCALE).then_inc(S[p + "h"], 1)
+    se.activation(hb[:, 4 * k + 3:4 * n:4], z1[:, k:n], ActivationFunctionType.Relu, scale=-SCALE).then_inc(S[p + "h"], 1)
     ve.wait_ge(S[p + "h"], 4)
     ve.quantize_mx(hq[:, 0:n], hs[:, 0:n], hb[:, 0:4 * n]).then_inc(S[p + "q"], 1)
     te.wait_ge(S.qw2, 1)
@@ -167,57 +242,86 @@ def rank_program(g, core, T, topo):
     rank = T.rank_of(core)
     if rank is None:
         return
-    sends, due, off, pos, late = _plan(T, topo)
+    sends, relays, due, off, pos, late, pad, win = _plan(T, topo)
     S = T.sem
     cnt = T.tables["CNT"]
     n = len(cnt)
     own = cnt[rank][rank]
     before = sum(cnt[i][rank] for i in range(rank))
-    landed = COLS - own
     tail = sum(cnt[j][rank] for j in late[rank])
-    head = landed - tail
+    head = COLS - own - tail + pad[rank]
+    landed = head + tail
     early = [j for j in range(n) if j != rank and j not in late[rank]]
+    ahead = win[rank]
+    split = bool(tail) and head >= WIN
+    spare = max(WIN, tail) - tail if split else 0
 
+    if ahead is not None:
+        g.sync.dma_start(T.ab[:], T.x[:, 4 * ahead:4 * (ahead + WIN)]).then_inc(S.la, 16)
     g.sync.dma_start(T.xb[:], T.x[:]).then_inc(S.lx, 16)
     g.sync.dma_start(T.w1b[:], T.w1[:]).then_inc(S.lw1, 16)
     g.sync.dma_start(T.w2b[:], T.w2[:]).then_inc(S.lw2, 16)
+    if spare:
+        g.vector.memset(T.lb[:, 0:4 * spare], 0.0).then_inc(S.zl, 1)
+    if ahead is not None:
+        g.vector.wait_ge(S.la, 16)
+        g.vector.quantize_mx(T.aq[:], T.asc[:], T.ab[:]).then_inc(S.qa, 1)
     g.vector.wait_ge(S.lx, 16)
     g.vector.quantize_mx(T.xq[:], T.xs[:], T.xb[:]).then_inc(S.qx, 1)
     g.vector.wait_ge(S.lw1, 16)
     g.vector.quantize_mx(T.w1q[:], T.w1s[:], T.w1b[:]).then_inc(S.qw1, 1)
     g.vector.wait_ge(S.lw2, 16)
     g.vector.quantize_mx(T.w2q[:], T.w2s[:], T.w2b[:]).then_inc(S.qw2, 1)
+    if spare:
+        g.vector.wait_ge(S.zl, 1)
 
+    left = 0
+    if ahead is not None:
+        g.wait_ge(S.qa, 1)
+        left += _send(g, core, T, topo, sends[core][0])
     g.wait_ge(S.qx, 1)
-    left = _send(g, core, T, topo, sends[core][0])
     left += _send(g, core, T, topo, sends[core][1])
-    if sends[core][2]:
-        g.wait_ge(S.run, due[core]["run"])
-        left += _send(g, core, T, topo, sends[core][2])
+    for width, slot, steps in relays[core]:
+        for sem, calls in steps:
+            g.wait_ge(S[sem], due[core][sem])
+            left += _send(g, core, T, topo, calls)
     g.wait_ge(S.sent, left)
 
-    copies = 0
+    first_sem = S.ye if split else S.yc
+    firsts, copies = 0, 0
     if own:
         assert own <= WIN
         first = min(off[rank][rank], COLS - WIN)
         g.tensor.wait_ge(S.qx, 1)
         _expert(g, T, "o", T.xq[:, first:first + WIN], T.xs[:, first:first + WIN], WIN, T.oz0, T.oz1, T.ob, T.ocq, T.ocs, T.op)
         at = off[rank][rank] - first
-        g.vector.tensor_copy(T.yb[:, before:before + own], T.op[:, at:at + own]).then_inc(S.yc, 1)
-        copies += 1
+        g.vector.tensor_copy(T.yb[:, before:before + own], T.op[:, at:at + own]).then_inc(first_sem, 1)
+        firsts += 1
     g.tensor.wait_ge(S.arr, due[core]["arr"])
-    if tail and head >= WIN:
+    if split:
         _expert(g, T, "m", T.bq[:, 0:head], T.bs[:, 0:head], head, T.mz0, T.mz1, T.hb, T.hq, T.hs, T.mp)
         for ya, sa, w in _pieces(early, cnt, rank, pos, 0):
-            g.vector.tensor_copy(T.yb[:, ya:ya + w], T.mp[:, sa:sa + w]).then_inc(S.yc, 1)
-            copies += 1
-        wide = max(WIN, tail)
+            g.vector.tensor_copy(T.yb[:, ya:ya + w], T.mp[:, sa:sa + w]).then_inc(S.ye, 1)
+            firsts += 1
+        wide = tail + spare
         a = landed - wide
         g.tensor.wait_ge(S.arl, due[core]["arl"])
-        _expert(g, T, "v", T.bq[:, a:landed], T.bs[:, a:landed], wide, T.oz0, T.oz1, T.lb, T.lcq, T.lcs, T.lp)
-        for ya, sa, w in _pieces(late[rank], cnt, rank, pos, a):
+        _expert(g, T, "v", T.bq[:, a:landed], T.bs[:, a:landed], wide, T.oz0, T.oz1, T.lb, T.lcq, T.lcs, T.lp, spare)
+        last = _pieces(late[rank], cnt, rank, pos, a)
+        for ya, sa, w in last:
             g.vector.tensor_copy(T.yb[:, ya:ya + w], T.lp[:, sa:sa + w]).then_inc(S.yc, 1)
             copies += 1
+        lo, hi = min(p[0] for p in last), max(p[0] + p[2] for p in last)
+        assert hi - lo == tail
+        sides = [(p, q) for p, q in ((0, lo), (hi, COLS)) if q > p]
+        g.sync.wait_ge(S.ye, firsts)
+        for p, q in sides:
+            g.sync.dma_start(T.y[:, p:q], T.yb[:, p:q]).then_inc(S.se, 16)
+        g.sync.wait_ge(S.yc, copies)
+        g.sync.dma_start(T.y[:, lo:hi], T.yb[:, lo:hi]).then_inc(S.st, 16)
+        g.sync.wait_ge(S.st, 16)
+        if sides:
+            g.sync.wait_ge(S.se, 16 * len(sides))
     else:
         if tail:
             g.tensor.wait_ge(S.arl, due[core]["arl"])
@@ -225,6 +329,6 @@ def rank_program(g, core, T, topo):
         for ya, sa, w in _pieces(early + late[rank], cnt, rank, pos, 0):
             g.vector.tensor_copy(T.yb[:, ya:ya + w], T.mp[:, sa:sa + w]).then_inc(S.yc, 1)
             copies += 1
-    g.sync.wait_ge(S.yc, copies)
-    g.sync.dma_start(T.y[:], T.yb[:]).then_inc(S.st, 16)
-    g.sync.wait_ge(S.st, 16)
+        g.sync.wait_ge(S.yc, firsts + copies)
+        g.sync.dma_start(T.y[:], T.yb[:]).then_inc(S.st, 16)
+        g.sync.wait_ge(S.st, 16)

import numpy
from concourse.bass import DstId, RemoteDMATransfer
from concourse.mybir import dt, AluOpType, ActivationFunctionType

COLS = 256
WIN = 128
SCALE = float(numpy.float32(0.043))

SCRATCH = {
    "ab": ("sbuf", [128, 4 * WIN], "bfloat16"),
    "aq": ("sbuf", [128, WIN], "float8_e4m3fn_x4"), "asc": ("sbuf", [128, WIN], "uint8"),
    "xb": ("sbuf", [128, 4 * COLS], "bfloat16"),
    "w1b": ("sbuf", [128, 1024], "bfloat16"),
    "w2b": ("sbuf", [128, 512], "bfloat16"),
    "xq": ("sbuf", [128, COLS], "float8_e4m3fn_x4"), "xs": ("sbuf", [128, COLS], "uint8"),
    "w1q": ("sbuf", [128, 256], "float8_e4m3fn_x4"), "w1s": ("sbuf", [128, 256], "uint8"),
    "w2q": ("sbuf", [128, 128], "float8_e4m3fn_x4"), "w2s": ("sbuf", [128, 128], "uint8"),
    "bq": ("sbuf", [128, COLS], "float8_e4m3fn_x4"), "bs": ("sbuf", [128, COLS], "uint8"),
    "tq": ("sbuf", [128, 4 * COLS], "float8_e4m3fn_x4"), "ts": ("sbuf", [128, 4 * COLS], "uint8"),
    "hb": ("sbuf", [128, 4 * COLS], "bfloat16"),
    "hq": ("sbuf", [128, COLS], "float8_e4m3fn_x4"), "hs": ("sbuf", [128, COLS], "uint8"),
    "lb": ("sbuf", [128, 4 * COLS], "bfloat16"),
    "lcq": ("sbuf", [128, COLS], "float8_e4m3fn_x4"), "lcs": ("sbuf", [128, COLS], "uint8"),
    "ob": ("sbuf", [128, 4 * WIN], "bfloat16"),
    "ocq": ("sbuf", [128, WIN], "float8_e4m3fn_x4"), "ocs": ("sbuf", [128, WIN], "uint8"),
    "yb": ("sbuf", [128, COLS], "float32"),
    "mz0": ("psum", [128, 512], "float32"), "mz1": ("psum", [128, 512], "float32"), "mp": ("psum", [128, 512], "float32"),
    "oz0": ("psum", [128, 512], "float32"), "oz1": ("psum", [128, 512], "float32"), "op": ("psum", [128, 512], "float32"),
    "lp": ("psum", [128, 512], "float32"),
}
RUNS = 4
SEMAPHORES = ["la", "lx", "lw1", "lw2", "qa", "qx", "qw1", "qw2", "sent", "arr", "arl", "zl"] + [
              "r%s%d" % (t, k) for k in range(RUNS) for t in "cs"] + [
              "m0", "m1", "mh", "mq", "mpp", "o0", "o1", "oh", "oq", "opp", "v0", "v1", "vh", "vq", "vpp", "ye", "yc", "se", "st"]

_CACHE = {}


def _engines(mask):
    return sum((mask >> b) & 1 for b in range(mask.bit_length()))


def _halves(mask):
    bits = [b for b in range(mask.bit_length()) if (mask >> b) & 1]
    half = len(bits) // 2
    return [sum(1 << b for b in bits[:half]), sum(1 << b for b in bits[half:])]


def _width(t):
    return t[3] * (4 if t[0] == "c" else 1)


def _fuse(todo):
    calls, used = [], set()
    for i in range(len(todo) - 1, -1, -1):
        if i in used:
            continue
        by = {}
        for k in range(i, -1, -1):
            m = todo[k][8]
            if k in used or _width(todo[k]) != _width(todo[i]) or any(m != o and m & o for o in by):
                continue
            if len(by.setdefault(m, [])) < 2:
                by[m].append(k)
        call = []
        for m, ks in by.items():
            for k, part in zip(ks, _halves(m) if len(ks) == 2 else [m]):
                call.append(todo[k][:8] + (part,))
                used.add(k)
        calls.append(call)
    return calls[::-1]


def _plan(T, topo):
    if "p" in _CACHE:
        return _CACHE["p"]
    cores = list(T.cores)
    n = len(cores)
    cnt = T.tables["CNT"]
    off = [[sum(r[:e]) for e in range(n + 1)] for r in cnt]

    def one_chip(a, b):
        return topo.host(a) == topo.host(b) and topo.chip(a) == topo.chip(b)

    late = [[j for j in range(n) if j != e and cnt[j][e] and not topo.may_write(cores[j], cores[e])] for e in range(n)]
    pos, pad, wide = [], [0] * n, {}
    for e in range(n):
        near = [j for j in range(n) if j != e and j not in late[e] and one_chip(cores[j], cores[e]) and cnt[j][e]]
        first = [j for j in range(n) if j != e and j not in late[e] and j not in near]
        head = sum(cnt[j][e] for j in first + near)
        if late[e] and head < WIN and near:
            pad[e] = WIN - head
        at, row = 0, [0] * n
        for j in first + near + late[e]:
            row[j] = at
            if pad[e] and j == near[-1]:
                w = cnt[j][e] + pad[e]
                if off[j][e] + w <= COLS:
                    wide[(j, e)] = (off[j][e], w, at)
                else:
                    assert off[j][e + 1] - w >= 0
                    wide[(j, e)] = (off[j][e + 1] - w, w, at)
                    row[j] = at + pad[e]
                at += w
            else:
                at += cnt[j][e]
        assert at <= COLS
        pos.append(row)
    sends, relays, due = {c: [[], [], []] for c in cores}, {c: [] for c in cores}, {}
    buf = {"c": ("xq", "tq", "bq", "aq"), "s": ("xs", "ts", "bs", "asc")}

    def put(todo, kind, sb, a, w, dst, db, da, sem, mask):
        if w == 0:
            return
        todo.append((kind, sb, a, w, dst, db, da, sem, mask))

    groups = []
    for j, c in enumerate(cores):
        others = [e for e in range(n) if e != j]
        chip = [e for e in others if one_chip(c, cores[e])]
        diag = [e for e in others if not topo.may_write(c, cores[e])]
        straight = [e for e in others if e not in chip and e not in diag]
        assert diag == list(range(diag[0], diag[-1] + 1))
        straight.sort(key=lambda e: (topo.same_plane(c, cores[e]), e))
        groups.append((chip, diag, straight))
    load = [2 * sum(1 for e in groups[j][2] if cnt[j][e]) + 2 * (1 if any(cnt[j][e] for e in groups[j][1]) else 0)
            for j in range(n)]
    relay_of, room = {}, [0] * n
    todo = sorted(range(n), key=lambda j: (-sum(1 for e in groups[j][1] if cnt[j][e]), j))
    for j in todo:
        chip, diag, straight = groups[j]
        pieces = 2 * sum(1 for e in diag if cnt[j][e])
        if not pieces:
            continue
        can = [r for r in straight if all(topo.may_write(cores[r], cores[e]) for e in diag)]
        r = min(can, key=lambda r: (load[r], topo.same_plane(cores[j], cores[r]), r))
        relay_of[j] = r
        load[r] += pieces

    win = [None] * n
    for j, c in enumerate(cores):
        chip, diag, straight = groups[j]
        far = topo.mask(c, cores[straight[0]])
        if j in relay_of:
            r = relay_of[j]
            relay = cores[r]
            live = [e for e in diag if cnt[j][e]]
            a, b = off[j][live[0]], off[j][live[-1] + 1]
            assert b - a <= WIN
            win[j] = min(a, COLS - WIN)
            base = room[r]
            room[r] += b - a
            assert room[r] <= 4 * COLS and len(relays[relay]) < RUNS
            slot = len(relays[relay])
            for kind in ("c", "s"):
                put(sends[c][0], kind, buf[kind][3], a - win[j], b - a, relay, buf[kind][1], base, "r%s%d" % (kind, slot),
                    topo.mask(c, relay))
            on = []
            for e in sorted(live, key=lambda e: (-sum(cnt[i][e] for i in late[e]), e)):
                for kind in ("c", "s"):
                    put(on, kind, buf[kind][1], base + off[j][e] - a, cnt[j][e], cores[e], buf[kind][2], pos[e][j], "arl",
                        topo.mask(relay, cores[e]))
            relays[relay].append((b - a, slot, [("rc%d" % slot, [[t] for t in on[:1]]), ("rs%d" % slot, [[t] for t in on[1:]])]))
        for e in straight:
            for kind in ("c", "s"):
                put(sends[c][1], kind, buf[kind][0], off[j][e], cnt[j][e], cores[e], buf[kind][2], pos[e][j], "arr",
                    topo.mask(c, cores[e]))
        for e in chip:
            near = topo.mask(c, cores[e]) & ~far
            a, w, da = wide.get((j, e), (off[j][e], cnt[j][e], pos[e][j]))
            for kind in ("c", "s"):
                put(sends[c][2], kind, buf[kind][0], a, w, cores[e], buf[kind][2], da, "arr",
                    near if near else topo.mask(c, cores[e]))
    for c in cores:
        relays[c].sort(key=lambda t: (t[0], t[1]))
        sends[c] = [[[t] for t in sends[c][0]], _fuse(sends[c][1] + sends[c][2])]
        for calls in sends[c] + [s[1] for r in relays[c] for s in r[2]]:
            for call in calls:
                for t in call:
                    d = due.setdefault(t[4], {})
                    d[t[7]] = d.get(t[7], 0) + _engines(t[8])
    _CACHE["p"] = (sends, relays, due, off, pos, late, pad, win)
    return _CACHE["p"]


def _send(g, core, T, topo, calls):
    left = 0
    for call in calls:
        parts = []
        for kind, sb, a, w, dst, db, da, sem, mask in call:
            src, out = T[sb][:, a:a + w], T[db][:, da:da + w]
            if kind == "c":
                src, out = src.bitcast(dt.uint8), out.bitcast(dt.uint8)
            rid, pid = topo.addr(dst, core)
            parts.append((src, out, rid, pid, T.sem[sem], mask))
            left += _engines(mask)
        if len(parts) == 1:
            src, out, rid, pid, sem, mask = parts[0]
            g.remote_dma(out_ap=out, in_ap=src, remote_sem=sem, local_sem=T.sem.sent, pid=pid, routing_id=rid,
                         dma_engine_mask=mask)
        else:
            g.remote_dma_fused([RemoteDMATransfer(dst_ids=[DstId(rid=rid, pnc=pid)], dma_engine_mask=mask, remote_sem=sem,
                                                  src=src, dst=out) for src, out, rid, pid, sem, mask in parts],
                               local_sem=T.sem.sent)
    return left


def _expert(g, T, p, rhs, rhs_s, n, z0, z1, hb, hq, hs, out, k=0):
    S, te, ve, se = T.sem, g.tensor, g.vector, g.scalar
    te.wait_ge(S.qw1, 1)
    te.matmul_mx(z0[:, 0:n], T.w1q[:, 0:128], T.w1s[:, 0:128], rhs, rhs_s, True, True).then_inc(S[p + "0"], 1)
    te.matmul_mx(z1[:, 0:n], T.w1q[:, 128:256], T.w1s[:, 128:256], rhs, rhs_s, True, True).then_inc(S[p + "1"], 1)
    ve.wait_ge(S[p + "0"], 1)
    ve.tensor_scalar(hb[:, 4 * k:4 * n:4], z0[:, k:n], SCALE, 0.0, AluOpType.mult, AluOpType.max).then_inc(S[p + "h"], 1)
    ve.tensor_scalar(hb[:, 4 * k + 1:4 * n:4], z0[:, k:n], -SCALE, 0.0, AluOpType.mult, AluOpType.max).then_inc(S[p + "h"], 1)
    se.wait_ge(S[p + "1"], 1)
    se.activation(hb[:, 4 * k + 2:4 * n:4], z1[:, k:n], ActivationFunctionType.Relu, scale=SCALE).then_inc(S[p + "h"], 1)
    se.activation(hb[:, 4 * k + 3:4 * n:4], z1[:, k:n], ActivationFunctionType.Relu, scale=-SCALE).then_inc(S[p + "h"], 1)
    ve.wait_ge(S[p + "h"], 4)
    ve.quantize_mx(hq[:, 0:n], hs[:, 0:n], hb[:, 0:4 * n]).then_inc(S[p + "q"], 1)
    te.wait_ge(S.qw2, 1)
    te.wait_ge(S[p + "q"], 1)
    te.matmul_mx(out[:, 0:n], T.w2q[:, 0:128], T.w2s[:, 0:128], hq[:, 0:n], hs[:, 0:n], True, True).then_inc(S[p + "pp"], 1)
    ve.wait_ge(S[p + "pp"], 1)


def _pieces(ranks, cnt, e, pos, shift):
    out = []
    for j in ranks:
        w = cnt[j][e]
        if not w:
            continue
        ya, sa = sum(cnt[i][e] for i in range(j)), pos[e][j] - shift
        if out and out[-1][0] + out[-1][2] == ya and out[-1][1] + out[-1][2] == sa:
            out[-1] = (out[-1][0], out[-1][1], out[-1][2] + w)
        else:
            out.append((ya, sa, w))
    return out


def rank_program(g, core, T, topo):
    rank = T.rank_of(core)
    if rank is None:
        return
    sends, relays, due, off, pos, late, pad, win = _plan(T, topo)
    S = T.sem
    cnt = T.tables["CNT"]
    n = len(cnt)
    own = cnt[rank][rank]
    before = sum(cnt[i][rank] for i in range(rank))
    tail = sum(cnt[j][rank] for j in late[rank])
    head = COLS - own - tail + pad[rank]
    landed = head + tail
    early = [j for j in range(n) if j != rank and j not in late[rank]]
    ahead = win[rank]
    split = bool(tail) and head >= WIN
    spare = max(WIN, tail) - tail if split else 0

    if ahead is not None:
        g.sync.dma_start(T.ab[:], T.x[:, 4 * ahead:4 * (ahead + WIN)]).then_inc(S.la, 16)
    g.sync.dma_start(T.xb[:], T.x[:]).then_inc(S.lx, 16)
    g.sync.dma_start(T.w1b[:], T.w1[:]).then_inc(S.lw1, 16)
    g.sync.dma_start(T.w2b[:], T.w2[:]).then_inc(S.lw2, 16)
    if spare:
        g.vector.memset(T.lb[:, 0:4 * spare], 0.0).then_inc(S.zl, 1)
    if ahead is not None:
        g.vector.wait_ge(S.la, 16)
        g.vector.quantize_mx(T.aq[:], T.asc[:], T.ab[:]).then_inc(S.qa, 1)
    g.vector.wait_ge(S.lx, 16)
    g.vector.quantize_mx(T.xq[:], T.xs[:], T.xb[:]).then_inc(S.qx, 1)
    g.vector.wait_ge(S.lw1, 16)
    g.vector.quantize_mx(T.w1q[:], T.w1s[:], T.w1b[:]).then_inc(S.qw1, 1)
    g.vector.wait_ge(S.lw2, 16)
    g.vector.quantize_mx(T.w2q[:], T.w2s[:], T.w2b[:]).then_inc(S.qw2, 1)
    if spare:
        g.vector.wait_ge(S.zl, 1)

    left = 0
    if ahead is not None:
        g.wait_ge(S.qa, 1)
        left += _send(g, core, T, topo, sends[core][0])
    g.wait_ge(S.qx, 1)
    left += _send(g, core, T, topo, sends[core][1])
    for width, slot, steps in relays[core]:
        for sem, calls in steps:
            g.wait_ge(S[sem], due[core][sem])
            left += _send(g, core, T, topo, calls)
    g.wait_ge(S.sent, left)

    first_sem = S.ye if split else S.yc
    firsts, copies = 0, 0
    if own:
        assert own <= WIN
        first = min(off[rank][rank], COLS - WIN)
        g.tensor.wait_ge(S.qx, 1)
        _expert(g, T, "o", T.xq[:, first:first + WIN], T.xs[:, first:first + WIN], WIN, T.oz0, T.oz1, T.ob, T.ocq, T.ocs, T.op)
        at = off[rank][rank] - first
        g.vector.tensor_copy(T.yb[:, before:before + own], T.op[:, at:at + own]).then_inc(first_sem, 1)
        firsts += 1
    g.tensor.wait_ge(S.arr, due[core]["arr"])
    if split:
        _expert(g, T, "m", T.bq[:, 0:head], T.bs[:, 0:head], head, T.mz0, T.mz1, T.hb, T.hq, T.hs, T.mp)
        for ya, sa, w in _pieces(early, cnt, rank, pos, 0):
            g.vector.tensor_copy(T.yb[:, ya:ya + w], T.mp[:, sa:sa + w]).then_inc(S.ye, 1)
            firsts += 1
        wide = tail + spare
        a = landed - wide
        g.tensor.wait_ge(S.arl, due[core]["arl"])
        _expert(g, T, "v", T.bq[:, a:landed], T.bs[:, a:landed], wide, T.oz0, T.oz1, T.lb, T.lcq, T.lcs, T.lp, spare)
        last = _pieces(late[rank], cnt, rank, pos, a)
        for ya, sa, w in last:
            g.vector.tensor_copy(T.yb[:, ya:ya + w], T.lp[:, sa:sa + w]).then_inc(S.yc, 1)
            copies += 1
        lo, hi = min(p[0] for p in last), max(p[0] + p[2] for p in last)
        assert hi - lo == tail
        sides = [(p, q) for p, q in ((0, lo), (hi, COLS)) if q > p]
        g.sync.wait_ge(S.ye, firsts)
        for p, q in sides:
            g.sync.dma_start(T.y[:, p:q], T.yb[:, p:q]).then_inc(S.se, 16)
        g.sync.wait_ge(S.yc, copies)
        g.sync.dma_start(T.y[:, lo:hi], T.yb[:, lo:hi]).then_inc(S.st, 16)
        g.sync.wait_ge(S.st, 16)
        if sides:
            g.sync.wait_ge(S.se, 16 * len(sides))
    else:
        if tail:
            g.tensor.wait_ge(S.arl, due[core]["arl"])
        _expert(g, T, "m", T.bq[:, 0:landed], T.bs[:, 0:landed], landed, T.mz0, T.mz1, T.hb, T.hq, T.hs, T.mp)
        for ya, sa, w in _pieces(early + late[rank], cnt, rank, pos, 0):
            g.vector.tensor_copy(T.yb[:, ya:ya + w], T.mp[:, sa:sa + w]).then_inc(S.yc, 1)
            copies += 1
        g.sync.wait_ge(S.yc, firsts + copies)
        g.sync.dma_start(T.y[:], T.yb[:]).then_inc(S.st, 16)
        g.sync.wait_ge(S.st, 16)
